import numpy as np
import ml_dtypes


def mxq(x, axis, fmt="e4m3"):
    dtype, down = {"e4m3": (ml_dtypes.float8_e4m3fn, 7), "e5m2": (ml_dtypes.float8_e5m2, 14)}[fmt]
    v = np.moveaxis(np.asarray(x, np.float32).astype(ml_dtypes.bfloat16).astype(np.float64), axis, -1)
    blocks = v.reshape(v.shape[:-1] + (-1, 32))
    amax = np.abs(blocks).max(-1, keepdims=True)
    byte = np.maximum(np.where(amax > 0, np.frexp(amax)[1] - 1 + 127, 0) - down, 1)
    scale = np.exp2(byte - 127.0)
    codes = (blocks / scale).astype(np.float32).astype(dtype).astype(np.float64)
    return np.moveaxis((codes * scale).reshape(v.shape), -1, axis)


WIDE = False


def mx_kscale(k):
    if not WIDE:
        return np.ones(k)
    levels = np.array([10, -10, 5, -5, 0])
    if k % 512:
        return np.exp2(np.random.permutation(np.resize(levels, k // 32))).repeat(32)
    a = np.empty((k // 512, 16))
    for p in range(k // 512):
        a[p, :8] = np.random.permutation(np.resize(levels, 8))
        for g in range(8):
            far = levels[np.abs(levels - a[p, g]) >= 10]
            a[p, g + 8] = far[np.random.randint(len(far))]
    return np.exp2(a.ravel()).repeat(32)


def f64(x):
    return np.asarray(x).astype(np.float64)


E2M1 = np.array([0.0, 0.5, 1.0, 1.5, 2.0, 3.0, 4.0, 6.0, -0.0, -0.5, -1.0, -1.5, -2.0, -3.0, -4.0, -6.0])


def pack_weight(w, fmt):
    k, n = w.shape
    w = f64(np.asarray(w, np.float32).astype(ml_dtypes.bfloat16)).reshape(k // 32, 32, n)
    amax = np.abs(w).max(1)
    if fmt == "e4m3":
        byte = np.frexp(amax)[1] - 1 + 127 - 7
    else:
        mant, ex = np.frexp(amax / 6.0)
        byte = np.where(mant > 0.5, ex, ex - 1) + 127
    byte = np.clip(np.where(amax > 0, byte, 1), 1, 254)
    scaled = (w * np.exp2(127.0 - byte)[:, None, :]).reshape(k, n).astype(np.float32)
    by_word = np.ascontiguousarray(scaled.reshape(k // 512, 128, 4, n).transpose(0, 1, 3, 2))
    if fmt == "e4m3":
        words = by_word.astype(ml_dtypes.float8_e4m3fn).view(np.uint8)
    else:
        c = by_word.astype(ml_dtypes.float4_e2m1fn).view(np.uint8) & 0xF
        words = (c[..., 0::2] | (c[..., 1::2] << 4)).reshape(k // 512, 128, 2 * n)
    return np.ascontiguousarray(words), np.ascontiguousarray(byte.astype(np.uint8).reshape(k // 512, 16, n))


def unpack_weight(words, scales, fmt):
    g, _, n = scales.shape
    words = np.ascontiguousarray(words).reshape(g, 128, n, -1)
    if fmt == "e4m3":
        vals = words.view(ml_dtypes.float8_e4m3fn).astype(np.float64)
    else:
        nib = np.empty((g, 128, n, 4), np.uint8)
        nib[..., 0::2] = words & 0xF
        nib[..., 1::2] = words >> 4
        vals = E2M1[nib]
    vals = vals * np.repeat(np.exp2(scales.astype(np.float64) - 127.0), 8, axis=1)[..., None]
    return vals.transpose(0, 1, 3, 2).reshape(g * 512, n)


def bf(x):
    return np.asarray(x, np.float32).astype(ml_dtypes.bfloat16)


def planes(Y):
    r, m = Y.shape
    b = f64(bf(Y)).reshape(r // 32, 32, m)
    amax = np.abs(b).max(1)
    byte = np.clip(np.where(amax > 0, np.frexp(amax)[1] - 1 + 127 - 7, 1), 1, 254)
    codes = (b * np.exp2(127.0 - byte)[:, None, :]).reshape(r, m).astype(np.float32).astype(ml_dtypes.float8_e4m3fn).view(np.uint8)
    words = codes.reshape(r // 512, 128, 4, m).transpose(0, 1, 3, 2)
    return np.ascontiguousarray(words), np.ascontiguousarray(byte.astype(np.uint8).reshape(r // 512, 16, m))


K, L, T, R, N = 1024, 512, 512, 512, 512


def setup_inputs():
    n = np.random.standard_normal
    fk = mx_kscale(K)
    fl = mx_kscale(L)
    fr = mx_kscale(R)
    xtp = pack_weight(n((K, T)) / fk[:, None], "e2m1")
    wap = pack_weight(n((K, R)) * 1 / np.sqrt(K) * fk[:, None], "e4m3")
    xqp = pack_weight(n((L, T)) / fl[:, None], "e2m1")
    wcp = pack_weight(n((L, R)) * 1 / np.sqrt(L) * fl[:, None], "e4m3")
    wbp = pack_weight(n((R, N)) * 1 / np.sqrt(R) / fr[:, None], "e2m1")
    wyp = pack_weight(n((K, N)) * 0.6 / np.sqrt(K) * fk[:, None], "e4m3")
    return {
        "xt_words": xtp[0],
        "xt_scales": xtp[1],
        "wa_words": wap[0],
        "wa_scales": wap[1],
        "xq_words": xqp[0],
        "xq_scales": xqp[1],
        "wc_words": wcp[0],
        "wc_scales": wcp[1],
        "us": (np.random.uniform(0.5, 2.0, (R, 1)) * fr[:, None]).astype(np.float32),
        "wb_words": wbp[0],
        "wb_scales": wbp[1],
        "wy_words": wyp[0],
        "wy_scales": wyp[1],
    }


def reference(xt_words, xt_scales, wa_words, wa_scales, xq_words, xq_scales, wc_words, wc_scales, us, wb_words, wb_scales, wy_words, wy_scales):
    xtu = unpack_weight(xt_words, xt_scales, "e2m1")
    wau = unpack_weight(wa_words, wa_scales, "e4m3")
    xqu = unpack_weight(xq_words, xq_scales, "e2m1")
    wcu = unpack_weight(wc_words, wc_scales, "e4m3")
    wbu = unpack_weight(wb_words, wb_scales, "e2m1")
    wyu = unpack_weight(wy_words, wy_scales, "e4m3")
    z = wau.T @ xtu + wcu.T @ xqu
    zp = np.pad(z, ((0, 0), (1, 0)))[:, :T]
    hid = z * np.tanh(zp) * f64(us)
    hidq = mxq(hid, 0, "e4m3")
    y = wbu.T @ hidq + wyu.T @ xtu
    words, scales = planes(y)
    return y, words, scales

@@ -1,0 +1,277 @@
+from contextlib import ExitStack
+
+import concourse.mybir as mybir
+
+K, L, T, R, N = 1024, 512, 512, 512, 512
+FLOPS = 2 * T * (K * R + L * R + R * N + K * N)
+
+F32 = mybir.dt.float32
+BF16 = mybir.dt.bfloat16
+I32 = mybir.dt.int32
+U8 = mybir.dt.uint8
+FP8X4 = mybir.dt.float8_e4m3fn_x4
+FP4X4 = mybir.dt.float4_e2m1fn_x4
+ACT = mybir.ActivationFunctionType
+ALU = mybir.AluOpType
+
+P = 128
+PACK = 4
+COLS = 512
+TC = 128
+CHUNKS = T // TC
+PAD = 4
+
+
+def tile_mix_hidden_pairs_multiplied_pl_kernel(
+    tc, xt_words, xt_scales, wa_words, wa_scales, xq_words, xq_scales, wc_words, wc_scales, us,
+    wb_words, wb_scales, wy_words, wy_scales, out_0, out_1, out_2,
+):
+    nc = tc.nc
+    with ExitStack() as ctx:
+        sb = ctx.enter_context(tc.tile_pool(name="sb", bufs=1))
+        ps = ctx.enter_context(tc.psum_pool(name="ps", bufs=1))
+        ctx.enter_context(tc.manual_schedule())
+
+        def tile(name, width, dtype):
+            return sb.tile([P, width], dtype, name=name, align_bytes=64)
+
+        xt_w = tile("xt_w", 2 * 2 * COLS, U8)
+        xq_w = tile("xq_w", 2 * COLS, U8)
+        wa_raw = tile("wa_raw", 2 * COLS, I32)
+        wc_raw = tile("wc_raw", COLS, I32)
+        wy_raw = tile("wy_raw", 2 * COLS, I32)
+        wb_raw = tile("wb_raw", 2 * COLS, U8)
+        wa_w = tile("wa_w", 2 * COLS, I32)
+        wc_w = tile("wc_w", COLS, I32)
+        wy_w = tile("wy_w", 2 * COLS, I32)
+        wb_w = tile("wb_w", 2 * COLS, U8)
+        first_s = tile("first_s", 4 * COLS, U8)
+        second_s = tile("second_s", 2 * COLS, U8)
+        third_s = tile("third_s", 3 * COLS, U8)
+        wa_sraw, xt_s = first_s[:, 0:2 * COLS], first_s[:, 2 * COLS:4 * COLS]
+        wc_sraw, xq_s = second_s[:, 0:COLS], second_s[:, COLS:2 * COLS]
+        wy_sraw, wb_sraw = third_s[:, 0:2 * COLS], third_s[:, 2 * COLS:3 * COLS]
+        wa_s = tile("wa_s", 2 * COLS, U8)
+        wc_s = tile("wc_s", COLS, U8)
+        wy_s = tile("wy_s", 2 * COLS, U8)
+        wb_s = tile("wb_s", COLS, U8)
+        us_sb = tile("us_sb", PACK, F32)
+        zero = tile("zero", PACK, F32)
+        th = sb.tile([P, PACK, PAD + T], F32, name="th", align_bytes=64)
+        hid32 = [tile("hid32_%d" % c, PACK * TC, F32) for c in range(CHUNKS)]
+        hid16 = [tile("hid16_%d" % c, PACK * TC, BF16) for c in range(CHUNKS)]
+        hid_w = [tile("hid_w_%d" % c, TC, I32) for c in range(CHUNKS)]
+        hid_s = [tile("hid_s_%d" % c, TC, U8) for c in range(CHUNKS)]
+        y32 = [tile("y32_%d" % c, PACK * TC, F32) for c in range(CHUNKS)]
+        y16 = [tile("y16_%d" % c, PACK * TC, BF16) for c in range(CHUNKS)]
+        y_w = tile("y_w", T, I32)
+        y_s = tile("y_s", T, U8)
+        z_ps = [ps.tile([P, PACK * TC], F32, name="z_ps_%d" % c) for c in range(CHUNKS)]
+        y_ps = [ps.tile([P, PACK * TC], F32, name="y_ps_%d" % c) for c in range(CHUNKS)]
+
+        def load_words(queue, dst, words):
+            passes = words.shape[0]
+            if words.ndim == 4:
+                src = words.rearrange("z p n t -> p z (n t)").bitcast(I32)
+                dst32 = dst[:]
+            else:
+                src = words.rearrange("z p b -> p z b").bitcast(I32)
+                dst32 = dst[:].bitcast(I32)
+            queue.dma_start(out=dst32.rearrange("p (z n) -> p z n", z=passes), in_=src)
+
+        def load_scales(queue, plane, scales, q):
+            passes = scales.shape[0]
+            src = scales[:, 4 * q:4 * q + 4, :].rearrange("z r c -> r z c").bitcast(I32)
+            dst = plane.bitcast(I32)[32 * q:32 * q + 4, :].rearrange("r (z c) -> r z c", z=passes)
+            queue.dma_start(out=dst, in_=src)
+
+        def deal_words(dst, raw, z):
+            cols = slice(z * COLS, (z + 1) * COLS)
+            nc.vector.tensor_copy(
+                out=dst[:, cols].rearrange("p (j a b) -> p a j b", j=PACK, b=4),
+                in_=raw[:, cols].rearrange("p (a b j) -> p a j b", j=PACK, b=4),
+            )
+
+        def deal_scales(dst, raw):
+            nc.vector.tensor_copy(
+                out=dst[:].rearrange("p (z j m) -> p z j m", j=PACK, m=P),
+                in_=raw.rearrange("p (z m j) -> p z j m", j=PACK, m=P),
+            )
+
+        def deal_fp4_words(dst, raw):
+            nc.vector.tensor_copy(
+                out=dst[:].rearrange("p (j m b) -> p j m b", j=PACK, b=2),
+                in_=raw[:].rearrange("p (m j b) -> p j m b", j=PACK, b=2),
+            )
+
+        def fp8_by_fp4(bank, c, w_words, w_scales, x_words, x_scales, z, start, stop):
+            for j in range(PACK):
+                w0 = z * COLS + j * P
+                x0 = z * COLS + c * TC
+                nc.tensor.matmul_mx(
+                    out=bank[:, j * TC:(j + 1) * TC],
+                    lhsT=w_words[:, w0:w0 + P].bitcast(FP8X4),
+                    lhsT_scale=w_scales[:, w0:w0 + P],
+                    rhs=x_words[:, 2 * x0:2 * (x0 + TC)].bitcast(FP4X4),
+                    rhs_scale=x_scales[:, x0:x0 + TC],
+                    start=(start and j == 0),
+                    stop=(stop and j == PACK - 1),
+                )
+
+        def second_layer(c):
+            for j in range(PACK):
+                nc.tensor.matmul_mx(
+                    out=y_ps[c][:, j * TC:(j + 1) * TC],
+                    lhsT=wb_w[:, 2 * j * P:2 * (j + 1) * P].bitcast(FP4X4),
+                    lhsT_scale=wb_s[:, j * P:(j + 1) * P],
+                    rhs=hid_w[c][:].bitcast(FP8X4),
+                    rhs_scale=hid_s[c][:],
+                    start=False,
+                    stop=(j == PACK - 1),
+                )
+
+        def interleave(dst16, src32):
+            return dict(
+                out=dst16[:].rearrange("p (a b j) -> p a j b", j=PACK, b=4),
+                in_=src32[:].rearrange("p (j a b) -> p a j b", j=PACK, b=4),
+            )
+
+        def tanh(c):
+            nc.scalar.activation(
+                out=th[:, :, PAD + c * TC:PAD + (c + 1) * TC],
+                in_=z_ps[c][:].rearrange("p (j t) -> p j t", j=PACK),
+                func=ACT.Tanh,
+            )
+
+        def product(c):
+            for j in range(PACK):
+                nc.vector.scalar_tensor_tensor(
+                    out=hid32[c][:, j * TC:(j + 1) * TC],
+                    in0=z_ps[c][:, j * TC:(j + 1) * TC],
+                    scalar=us_sb[:, j:j + 1],
+                    in1=th[:, j, PAD - 1 + c * TC:PAD - 1 + (c + 1) * TC],
+                    op0=ALU.mult,
+                    op1=ALU.mult,
+                )
+
+        def round_hid(c):
+            nc.scalar.copy(**interleave(hid16[c], hid32[c]))
+
+        def quantize_hid(c):
+            nc.vector.quantize_mx(out=hid_w[c][:].bitcast(FP8X4), scales=hid_s[c][:], in_=hid16[c][:])
+
+        def drain_y(c):
+            nc.scalar.copy(out=y32[c][:], in_=y_ps[c][:])
+            nc.sync.dma_start(
+                out=out_0.rearrange("(p i) t -> p i t", i=PACK)[:, :, c * TC:(c + 1) * TC],
+                in_=y32[c][:].rearrange("p (i t) -> p i t", i=PACK),
+            )
+
+        def round_y(c):
+            nc.vector.tensor_copy(**interleave(y16[c], y32[c]))
+
+        def quantize_y(c):
+            cols = slice(c * TC, (c + 1) * TC)
+            nc.vector.quantize_mx(out=y_w[:, cols].bitcast(FP8X4), scales=y_s[:, cols], in_=y16[c][:])
+
+        nc.vector.memset(first_s[:].bitcast(I32), 0)
+        nc.vector.memset(second_s[:].bitcast(I32), 0)
+        nc.vector.memset(third_s[:].bitcast(I32), 0)
+        nc.vector.memset(zero[:], 0.0)
+
+        load_words(nc.scalar, wa_raw, wa_words)
+        load_words(nc.scalar, xt_w, xt_words)
+        for q in range(4):
+            load_scales(nc.sync, wa_sraw, wa_scales, q)
+        for q in range(2):
+            load_scales(nc.sync, xt_s, xt_scales, q)
+        for q in range(2, 4):
+            load_scales(nc.gpsimd, xt_s, xt_scales, q)
+        nc.scalar.activation(out=th[:, :, PAD - 1:PAD], in_=zero[:].unsqueeze(2), func=ACT.Tanh)
+        for q in range(2):
+            load_scales(nc.scalar, xq_s, xq_scales, q)
+        for q in range(2, 4):
+            load_scales(nc.gpsimd, xq_s, xq_scales, q)
+        for q in range(4):
+            load_scales(nc.sync, wc_sraw, wc_scales, q)
+        load_words(nc.sync, wc_raw, wc_words)
+        load_words(nc.sync, xq_w, xq_words)
+        nc.scalar.dma_start(out=us_sb[:], in_=us.rearrange("(p j) o -> p (j o)", j=PACK))
+        load_scales(nc.scalar, wb_sraw, wb_scales, 0)
+        for q in range(1, 4):
+            load_scales(nc.gpsimd, wb_sraw, wb_scales, q)
+        for q in range(4):
+            load_scales(nc.sync, wy_sraw, wy_scales, q)
+        load_words(nc.sync, wy_raw, wy_words)
+        load_words(nc.sync, wb_raw, wb_words)
+
+        deal_scales(wa_s, wa_sraw)
+        deal_words(wa_w, wa_raw, 0)
+        deal_words(wa_w, wa_raw, 1)
+        deal_scales(wc_s, wc_sraw)
+        deal_words(wc_w, wc_raw, 0)
+
+        def tokens_part(c):
+            for z in range(2):
+                fp8_by_fp4(z_ps[c], c, wa_w, wa_s, xt_w, xt_s, z, z == 0, False)
+
+        def second_input_part(c):
+            fp8_by_fp4(z_ps[c], c, wc_w, wc_s, xq_w, xq_s, 0, False, True)
+            tanh(c)
+
+        def skip(c):
+            for z in range(2):
+                fp8_by_fp4(y_ps[c], c, wy_w, wy_s, xt_w, xt_s, z, z == 0, False)
+
+        tokens_part(0)
+        tokens_part(1)
+        second_input_part(0)
+        second_input_part(1)
+        deal_scales(wy_s, wy_sraw)
+        product(0)
+        round_hid(0)
+        tokens_part(2)
+        second_input_part(2)
+        deal_words(wy_w, wy_raw, 0)
+        deal_words(wy_w, wy_raw, 1)
+        product(1)
+        round_hid(1)
+        quantize_hid(0)
+        tokens_part(3)
+        second_input_part(3)
+        deal_scales(wb_s, wb_sraw)
+        deal_fp4_words(wb_w, wb_raw)
+        product(2)
+        round_hid(2)
+        quantize_hid(1)
+        product(3)
+        round_hid(3)
+        quantize_hid(2)
+        skip(0)
+        second_layer(0)
+        drain_y(0)
+        skip(1)
+        second_layer(1)
+        quantize_hid(3)
+        round_y(0)
+        drain_y(1)
+        skip(2)
+        second_layer(2)
+        round_y(1)
+        quantize_y(0)
+        drain_y(2)
+        skip(3)
+        second_layer(3)
+        round_y(2)
+        quantize_y(1)
+        drain_y(3)
+        quantize_y(2)
+        round_y(3)
+        quantize_y(3)
+        nc.sync.dma_start(out=out_1.rearrange("z p n t -> p (z n t)").bitcast(I32), in_=y_w[:])
+        for q in range(4):
+            queue = nc.scalar if q % 2 == 0 else nc.sync
+            queue.dma_start(
+                out=out_2[0, 4 * q:4 * q + 4, :].bitcast(I32),
+                in_=y_s[:].bitcast(I32)[32 * q:32 * q + 4, :],
+            )

@@ -56,7 +56,7 @@ def tile_mix_hidden_pairs_multiplied_pl_kernel(
         wy_s = tile("wy_s", 2 * COLS, U8)
         wb_s = tile("wb_s", COLS, U8)
         us_sb = tile("us_sb", PACK, F32)
-        zero = tile("zero", PACK, F32)
+        zero = tile("zero", PACK * TC, BF16)
         th = sb.tile([P, PACK, PAD + T], F32, name="th", align_bytes=64)
         hid32 = [tile("hid32_%d" % c, PACK * TC, F32) for c in range(CHUNKS)]
         hid16 = [tile("hid16_%d" % c, PACK * TC, BF16) for c in range(CHUNKS)]
@@ -154,8 +154,11 @@ def tile_mix_hidden_pairs_multiplied_pl_kernel(
                     op1=ALU.mult,
                 )
 
-        def round_hid(c):
-            nc.scalar.copy(**interleave(hid16[c], hid32[c]))
+        def round_hid(c, on_vector=False):
+            if on_vector:
+                nc.vector.tensor_copy(**interleave(hid16[c], hid32[c]))
+            else:
+                nc.scalar.copy(**interleave(hid16[c], hid32[c]))
 
         def quantize_hid(c):
             nc.vector.quantize_mx(out=hid_w[c][:].bitcast(FP8X4), scales=hid_s[c][:], in_=hid16[c][:])
@@ -176,40 +179,35 @@ def tile_mix_hidden_pairs_multiplied_pl_kernel(
 
         nc.vector.memset(first_s[:].bitcast(I32), 0)
         nc.vector.memset(second_s[:].bitcast(I32), 0)
-        nc.vector.memset(third_s[:].bitcast(I32), 0)
         nc.vector.memset(zero[:], 0.0)
+        nc.vector.memset(third_s[:].bitcast(I32), 0)
 
         load_words(nc.scalar, wa_raw, wa_words)
-        load_words(nc.scalar, xt_w, xt_words)
-        for q in range(4):
-            load_scales(nc.sync, wa_sraw, wa_scales, q)
-        for q in range(2):
-            load_scales(nc.sync, xt_s, xt_scales, q)
-        for q in range(2, 4):
-            load_scales(nc.gpsimd, xt_s, xt_scales, q)
-        nc.scalar.activation(out=th[:, :, PAD - 1:PAD], in_=zero[:].unsqueeze(2), func=ACT.Tanh)
-        for q in range(2):
-            load_scales(nc.scalar, xq_s, xq_scales, q)
-        for q in range(2, 4):
-            load_scales(nc.gpsimd, xq_s, xq_scales, q)
-        for q in range(4):
-            load_scales(nc.sync, wc_sraw, wc_scales, q)
+        load_words(nc.gpsimd, xt_w, xt_words)
+        load_words(nc.gpsimd, wy_raw, wy_words)
+        load_words(nc.gpsimd, wb_raw, wb_words)
+        nc.scalar.activation(out=th[:, :, PAD - 1:PAD], in_=zero[:, 0:PACK].unsqueeze(2), func=ACT.Tanh)
+        for plane, scales in ((wa_sraw, wa_scales), (xt_s, xt_scales), (wc_sraw, wc_scales)):
+            for q in range(4):
+                load_scales(nc.sync, plane, scales, q)
         load_words(nc.sync, wc_raw, wc_words)
         load_words(nc.sync, xq_w, xq_words)
-        nc.scalar.dma_start(out=us_sb[:], in_=us.rearrange("(p j) o -> p (j o)", j=PACK))
-        load_scales(nc.scalar, wb_sraw, wb_scales, 0)
-        for q in range(1, 4):
-            load_scales(nc.gpsimd, wb_sraw, wb_scales, q)
+        for plane, scales in ((xq_s, xq_scales), (wy_sraw, wy_scales)):
+            for q in range(4):
+                load_scales(nc.sync, plane, scales, q)
+        nc.sync.dma_start(out=us_sb[:], in_=us.rearrange("(p j) o -> p (j o)", j=PACK))
         for q in range(4):
-            load_scales(nc.sync, wy_sraw, wy_scales, q)
-        load_words(nc.sync, wy_raw, wy_words)
-        load_words(nc.sync, wb_raw, wb_words)
+            load_scales(nc.sync, wb_sraw, wb_scales, q)
 
         deal_scales(wa_s, wa_sraw)
         deal_words(wa_w, wa_raw, 0)
         deal_words(wa_w, wa_raw, 1)
         deal_scales(wc_s, wc_sraw)
         deal_words(wc_w, wc_raw, 0)
+        deal_words(wy_w, wy_raw, 0)
+        deal_words(wy_w, wy_raw, 1)
+        deal_fp4_words(wb_w, wb_raw)
+        deal_scales(wy_s, wy_sraw)
 
         def tokens_part(c):
             for z in range(2):
@@ -223,52 +221,53 @@ def tile_mix_hidden_pairs_multiplied_pl_kernel(
             for z in range(2):
                 fp8_by_fp4(y_ps[c], c, wy_w, wy_s, xt_w, xt_s, z, z == 0, False)
 
+        def store_words(c0, c1):
+            cols = slice(c0 * TC, c1 * TC)
+            nc.sync.dma_start(out=out_1.rearrange("z p n t -> p (z n t)").bitcast(I32)[:, cols], in_=y_w[:, cols])
+
         tokens_part(0)
         tokens_part(1)
         second_input_part(0)
         second_input_part(1)
-        deal_scales(wy_s, wy_sraw)
-        product(0)
-        round_hid(0)
         tokens_part(2)
         second_input_part(2)
-        deal_words(wy_w, wy_raw, 0)
-        deal_words(wy_w, wy_raw, 1)
-        product(1)
-        round_hid(1)
-        quantize_hid(0)
         tokens_part(3)
         second_input_part(3)
+        product(0)
+        product(1)
+        round_hid(0, True)
         deal_scales(wb_s, wb_sraw)
-        deal_fp4_words(wb_w, wb_raw)
+        quantize_hid(0)
         product(2)
+        round_hid(1)
+        product(3)
         round_hid(2)
         quantize_hid(1)
-        product(3)
-        round_hid(3)
-        quantize_hid(2)
+        round_hid(3, True)
         skip(0)
-        second_layer(0)
-        drain_y(0)
         skip(1)
-        second_layer(1)
-        quantize_hid(3)
-        round_y(0)
-        drain_y(1)
+        second_layer(0)
         skip(2)
+        second_layer(1)
+        quantize_hid(2)
+        drain_y(0)
+        quantize_hid(3)
+        drain_y(1)
         second_layer(2)
-        round_y(1)
-        quantize_y(0)
-        drain_y(2)
         skip(3)
         second_layer(3)
+        round_y(0)
+        drain_y(2)
+        round_y(1)
+        quantize_y(0)
+        drain_y(3)
         round_y(2)
         quantize_y(1)
-        drain_y(3)
-        quantize_y(2)
+        store_words(0, 2)
         round_y(3)
+        quantize_y(2)
         quantize_y(3)
-        nc.sync.dma_start(out=out_1.rearrange("z p n t -> p (z n t)").bitcast(I32), in_=y_w[:])
+        store_words(2, 4)
         for q in range(4):
             queue = nc.scalar if q % 2 == 0 else nc.sync
             queue.dma_start(

@@ -16,10 +16,15 @@ ALU = mybir.AluOpType
 
 P = 128
 PACK = 4
+QUADRANTS = 4
 COLS = 512
-TC = 128
-CHUNKS = T // TC
+CHUNK = 128
+CHUNKS = T // CHUNK
+LAST = CHUNKS - 1
+RUN = 4
 PAD = 4
+EARLY = 3
+WARM_PASSES = 28
 
 
 def tile_mix_hidden_pairs_multiplied_pl_kernel(
@@ -32,64 +37,69 @@ def tile_mix_hidden_pairs_multiplied_pl_kernel(
         ps = ctx.enter_context(tc.psum_pool(name="ps", bufs=1))
         ctx.enter_context(tc.manual_schedule())
 
-        def tile(name, width, dtype):
+        def row(name, width, dtype):
             return sb.tile([P, width], dtype, name=name, align_bytes=64)
 
-        xt_w = tile("xt_w", 2 * 2 * COLS, U8)
-        xq_w = tile("xq_w", 2 * COLS, U8)
-        wa_raw = tile("wa_raw", 2 * COLS, I32)
-        wc_raw = tile("wc_raw", COLS, I32)
-        wy_raw = tile("wy_raw", 2 * COLS, I32)
-        wb_raw = tile("wb_raw", 2 * COLS, U8)
-        wa_w = tile("wa_w", 2 * COLS, I32)
-        wc_w = tile("wc_w", COLS, I32)
-        wy_w = tile("wy_w", 2 * COLS, I32)
-        wb_w = tile("wb_w", 2 * COLS, U8)
-        first_s = tile("first_s", 4 * COLS, U8)
-        second_s = tile("second_s", 2 * COLS, U8)
-        third_s = tile("third_s", 3 * COLS, U8)
-        wa_sraw, xt_s = first_s[:, 0:2 * COLS], first_s[:, 2 * COLS:4 * COLS]
-        wc_sraw, xq_s = second_s[:, 0:COLS], second_s[:, COLS:2 * COLS]
-        wy_sraw, wb_sraw = third_s[:, 0:2 * COLS], third_s[:, 2 * COLS:3 * COLS]
-        wa_s = tile("wa_s", 2 * COLS, U8)
-        wc_s = tile("wc_s", COLS, U8)
-        wy_s = tile("wy_s", 2 * COLS, U8)
-        wb_s = tile("wb_s", COLS, U8)
-        us_sb = tile("us_sb", PACK, F32)
-        zero = tile("zero", PACK * TC, BF16)
+        xt_w = row("xt_w", 2 * 2 * COLS, U8)
+        xq_w = row("xq_w", 2 * COLS, U8)
+        wa_raw, wa_w = row("wa_raw", 2 * COLS, I32), row("wa_w", 2 * COLS, I32)
+        wc_raw, wc_w = row("wc_raw", COLS, I32), row("wc_w", COLS, I32)
+        wy_raw, wy_w = row("wy_raw", 2 * COLS, I32), row("wy_w", 2 * COLS, I32)
+        wb_raw, wb_w = row("wb_raw", 2 * COLS, U8), row("wb_w", 2 * COLS, U8)
+
+        widths = [2 * COLS, 2 * COLS, 2 * PACK * CHUNK, 2 * COLS, 2 * COLS, COLS]
+        starts = [sum(widths[:i]) for i in range(len(widths) + 1)]
+        zeroed = row("zeroed", starts[-1], U8)
+        wa_sraw, xt_s, zero_bytes, wc_xq_s, wy_sraw, wb_sraw = [
+            zeroed[:, starts[i]:starts[i + 1]] for i in range(len(widths))
+        ]
+        wc_sraw, xq_s = wc_xq_s[:, 0:COLS], wc_xq_s[:, COLS:2 * COLS]
+        zeros = zero_bytes.bitcast(BF16)
+        wa_s, wc_s = row("wa_s", 2 * COLS, U8), row("wc_s", COLS, U8)
+        wy_s, wb_s = row("wy_s", 2 * COLS, U8), row("wb_s", COLS, U8)
+        warm_w, warm_s = row("warm_w", CHUNK, I32), row("warm_s", CHUNK, U8)
+
+        us_sb = row("us_sb", PACK, F32)
         th = sb.tile([P, PACK, PAD + T], F32, name="th", align_bytes=64)
-        hid32 = [tile("hid32_%d" % c, PACK * TC, F32) for c in range(CHUNKS)]
-        hid16 = [tile("hid16_%d" % c, PACK * TC, BF16) for c in range(CHUNKS)]
-        hid_w = [tile("hid_w_%d" % c, TC, I32) for c in range(CHUNKS)]
-        hid_s = [tile("hid_s_%d" % c, TC, U8) for c in range(CHUNKS)]
-        y32 = [tile("y32_%d" % c, PACK * TC, F32) for c in range(CHUNKS)]
-        y16 = [tile("y16_%d" % c, PACK * TC, BF16) for c in range(CHUNKS)]
-        y_w = tile("y_w", T, I32)
-        y_s = tile("y_s", T, U8)
-        z_ps = [ps.tile([P, PACK * TC], F32, name="z_ps_%d" % c) for c in range(CHUNKS)]
-        y_ps = [ps.tile([P, PACK * TC], F32, name="y_ps_%d" % c) for c in range(CHUNKS)]
+        hid32 = [row("hid32_%d" % c, PACK * CHUNK, F32) for c in range(CHUNKS)]
+        hid16 = [row("hid16_%d" % c, PACK * CHUNK, BF16) for c in range(CHUNKS)]
+        hid_w = [row("hid_w_%d" % c, CHUNK, I32) for c in range(CHUNKS)]
+        hid_s = [row("hid_s_%d" % c, CHUNK, U8) for c in range(CHUNKS)]
+        y32 = [row("y32_%d" % c, PACK * CHUNK, F32) for c in range(CHUNKS)]
+        y16 = [row("y16_%d" % c, PACK * CHUNK, BF16) for c in range(CHUNKS)]
+        y_w, y_s = row("y_w", T, I32), row("y_s", T, U8)
+        z_ps = [ps.tile([P, PACK * CHUNK], F32, name="z_ps_%d" % c) for c in range(CHUNKS)]
+        y_ps = [ps.tile([P, PACK * CHUNK], F32, name="y_ps_%d" % c) for c in range(CHUNKS)]
 
-        def load_words(queue, dst, words):
-            passes = words.shape[0]
-            if words.ndim == 4:
-                src = words.rearrange("z p n t -> p z (n t)").bitcast(I32)
-                dst32 = dst[:]
-            else:
-                src = words.rearrange("z p b -> p z b").bitcast(I32)
-                dst32 = dst[:].bitcast(I32)
-            queue.dma_start(out=dst32.rearrange("p (z n) -> p z n", z=passes), in_=src)
+        def clear(i):
+            first, end = starts[i] // 4 + i % 2, starts[i + 1] // 4 + (i + 1) % 2
+            nc.vector.memset(zeroed[:].bitcast(I32)[:, first:end], 0)
 
-        def load_scales(queue, plane, scales, q):
-            passes = scales.shape[0]
-            src = scales[:, 4 * q:4 * q + 4, :].rearrange("z r c -> r z c").bitcast(I32)
-            dst = plane.bitcast(I32)[32 * q:32 * q + 4, :].rearrange("r (z c) -> r z c", z=passes)
-            queue.dma_start(out=dst, in_=src)
+        def load_fp8_words(queue, dst, words):
+            src = words.rearrange("z p n t -> p z (n t)").bitcast(I32)
+            queue.dma_start(out=dst[:].rearrange("p (z n) -> p z n", n=COLS), in_=src)
 
-        def deal_words(dst, raw, z):
-            cols = slice(z * COLS, (z + 1) * COLS)
+        def load_fp4_words(queue, dst, words):
+            src = words.rearrange("z p b -> p z b").bitcast(I32)
+            queue.dma_start(out=dst[:].bitcast(I32).rearrange("p (z n) -> p z n", n=COLS // 2), in_=src)
+
+        def load_scales(plane, scales):
+            for q in range(QUADRANTS):
+                src = scales[:, 4 * q:4 * q + 4, :].rearrange("z r c -> r z c").bitcast(I32)
+                dst = plane.bitcast(I32)[32 * q:32 * q + 4, :].rearrange("r (z c) -> r z c", c=COLS // 4)
+                nc.sync.dma_start(out=dst, in_=src)
+
+        def deal_fp8_words(dst, raw):
+            for c0 in range(0, raw.shape[1], COLS):
+                nc.vector.tensor_copy(
+                    out=dst[:, c0:c0 + COLS].rearrange("p (j a b) -> p a j b", j=PACK, b=RUN),
+                    in_=raw[:, c0:c0 + COLS].rearrange("p (a b j) -> p a j b", j=PACK, b=RUN),
+                )
+
+        def deal_fp4_words(dst, raw):
             nc.vector.tensor_copy(
-                out=dst[:, cols].rearrange("p (j a b) -> p a j b", j=PACK, b=4),
-                in_=raw[:, cols].rearrange("p (a b j) -> p a j b", j=PACK, b=4),
+                out=dst[:].rearrange("p (j m b) -> p j m b", j=PACK, b=2),
+                in_=raw[:].rearrange("p (m j b) -> p j m b", j=PACK, b=2),
             )
 
         def deal_scales(dst, raw):
@@ -98,30 +108,34 @@ def tile_mix_hidden_pairs_multiplied_pl_kernel(
                 in_=raw.rearrange("p (z m j) -> p z j m", j=PACK, m=P),
             )
 
-        def deal_fp4_words(dst, raw):
-            nc.vector.tensor_copy(
-                out=dst[:].rearrange("p (j m b) -> p j m b", j=PACK, b=2),
-                in_=raw[:].rearrange("p (m j b) -> p j m b", j=PACK, b=2),
-            )
+        def fp8_weights_by_fp4_tokens(bank, c, w_words, w_scales, x_words, x_scales, opens, closes):
+            passes = w_scales.shape[1] // COLS
+            for z in range(passes):
+                for j in range(PACK):
+                    w0, x0 = z * COLS + j * P, z * COLS + c * CHUNK
+                    nc.tensor.matmul_mx(
+                        out=bank[:, j * CHUNK:(j + 1) * CHUNK],
+                        lhsT=w_words[:, w0:w0 + P].bitcast(FP8X4),
+                        lhsT_scale=w_scales[:, w0:w0 + P],
+                        rhs=x_words[:, 2 * x0:2 * (x0 + CHUNK)].bitcast(FP4X4),
+                        rhs_scale=x_scales[:, x0:x0 + CHUNK],
+                        start=(opens and z == 0 and j == 0),
+                        stop=(closes and z == passes - 1 and j == PACK - 1),
+                    )
 
-        def fp8_by_fp4(bank, c, w_words, w_scales, x_words, x_scales, z, start, stop):
-            for j in range(PACK):
-                w0 = z * COLS + j * P
-                x0 = z * COLS + c * TC
-                nc.tensor.matmul_mx(
-                    out=bank[:, j * TC:(j + 1) * TC],
-                    lhsT=w_words[:, w0:w0 + P].bitcast(FP8X4),
-                    lhsT_scale=w_scales[:, w0:w0 + P],
-                    rhs=x_words[:, 2 * x0:2 * (x0 + TC)].bitcast(FP4X4),
-                    rhs_scale=x_scales[:, x0:x0 + TC],
-                    start=(start and j == 0),
-                    stop=(stop and j == PACK - 1),
-                )
+        def wa_passes(c):
+            fp8_weights_by_fp4_tokens(z_ps[c], c, wa_w, wa_s, xt_w, xt_s, True, False)
 
-        def second_layer(c):
+        def wc_passes(c):
+            fp8_weights_by_fp4_tokens(z_ps[c], c, wc_w, wc_s, xq_w, xq_s, False, True)
+
+        def wy_passes(c):
+            fp8_weights_by_fp4_tokens(y_ps[c], c, wy_w, wy_s, xt_w, xt_s, True, False)
+
+        def wb_passes(c):
             for j in range(PACK):
                 nc.tensor.matmul_mx(
-                    out=y_ps[c][:, j * TC:(j + 1) * TC],
+                    out=y_ps[c][:, j * CHUNK:(j + 1) * CHUNK],
                     lhsT=wb_w[:, 2 * j * P:2 * (j + 1) * P].bitcast(FP4X4),
                     lhsT_scale=wb_s[:, j * P:(j + 1) * P],
                     rhs=hid_w[c][:].bitcast(FP8X4),
@@ -130,145 +144,126 @@ def tile_mix_hidden_pairs_multiplied_pl_kernel(
                     stop=(j == PACK - 1),
                 )
 
-        def interleave(dst16, src32):
-            return dict(
-                out=dst16[:].rearrange("p (a b j) -> p a j b", j=PACK, b=4),
-                in_=src32[:].rearrange("p (j a b) -> p a j b", j=PACK, b=4),
+        def by_row(tile):
+            return tile[:].rearrange("p (j t) -> p j t", j=PACK)
+
+        def round_and_interleave(copy, dst16, src32, t0, t1):
+            runs = slice(t0 // RUN, t1 // RUN)
+            copy(
+                out=dst16[:].rearrange("p (a b j) -> p a j b", j=PACK, b=RUN)[:, runs],
+                in_=src32[:].rearrange("p (j a b) -> p a j b", j=PACK, b=RUN)[:, runs],
             )
 
         def tanh(c):
-            nc.scalar.activation(
-                out=th[:, :, PAD + c * TC:PAD + (c + 1) * TC],
-                in_=z_ps[c][:].rearrange("p (j t) -> p j t", j=PACK),
-                func=ACT.Tanh,
-            )
+            nc.scalar.activation(out=th[:, :, PAD + c * CHUNK:PAD + (c + 1) * CHUNK], in_=by_row(z_ps[c]), func=ACT.Tanh)
 
         def product(c):
             for j in range(PACK):
                 nc.vector.scalar_tensor_tensor(
-                    out=hid32[c][:, j * TC:(j + 1) * TC],
-                    in0=z_ps[c][:, j * TC:(j + 1) * TC],
+                    out=hid32[c][:, j * CHUNK:(j + 1) * CHUNK],
+                    in0=z_ps[c][:, j * CHUNK:(j + 1) * CHUNK],
                     scalar=us_sb[:, j:j + 1],
-                    in1=th[:, j, PAD - 1 + c * TC:PAD - 1 + (c + 1) * TC],
+                    in1=th[:, j, PAD - 1 + c * CHUNK:PAD - 1 + (c + 1) * CHUNK],
                     op0=ALU.mult,
                     op1=ALU.mult,
                 )
 
-        def round_hid(c, on_vector=False):
-            if on_vector:
-                nc.vector.tensor_copy(**interleave(hid16[c], hid32[c]))
-            else:
-                nc.scalar.copy(**interleave(hid16[c], hid32[c]))
+        def round_hid(c):
+            copy = nc.vector.tensor_copy if c == LAST else nc.scalar.copy
+            round_and_interleave(copy, hid16[c], hid32[c], 0, CHUNK)
 
         def quantize_hid(c):
             nc.vector.quantize_mx(out=hid_w[c][:].bitcast(FP8X4), scales=hid_s[c][:], in_=hid16[c][:])
 
+        def parts(c):
+            return [(0, CHUNK // 2), (CHUNK // 2, CHUNK)] if c == LAST else [(0, CHUNK)]
+
         def drain_y(c):
-            nc.scalar.copy(out=y32[c][:], in_=y_ps[c][:])
-            nc.sync.dma_start(
-                out=out_0.rearrange("(p i) t -> p i t", i=PACK)[:, :, c * TC:(c + 1) * TC],
-                in_=y32[c][:].rearrange("p (i t) -> p i t", i=PACK),
-            )
+            for t0, t1 in parts(c):
+                nc.scalar.copy(out=by_row(y32[c])[:, :, t0:t1], in_=by_row(y_ps[c])[:, :, t0:t1])
+            rows = out_0.rearrange("(p j) t -> p j t", j=PACK)
+            nc.sync.dma_start(out=rows[:, :, c * CHUNK:(c + 1) * CHUNK], in_=by_row(y32[c]))
 
         def round_y(c):
-            nc.vector.tensor_copy(**interleave(y16[c], y32[c]))
+            for t0, t1 in parts(c):
+                round_and_interleave(nc.vector.tensor_copy, y16[c], y32[c], t0, t1)
 
         def quantize_y(c):
-            cols = slice(c * TC, (c + 1) * TC)
-            nc.vector.quantize_mx(out=y_w[:, cols].bitcast(FP8X4), scales=y_s[:, cols], in_=y16[c][:])
+            for t0, t1 in parts(c):
+                cols = slice(c * CHUNK + t0, c * CHUNK + t1)
+                nc.vector.quantize_mx(
+                    out=y_w[:, cols].bitcast(FP8X4), scales=y_s[:, cols], in_=y16[c][:, PACK * t0:PACK * t1]
+                )
+            if c % 2 == 1:
+                cols = slice((c - 1) * CHUNK, (c + 1) * CHUNK)
+                nc.sync.dma_start(out=out_1.rearrange("z p n t -> p (z n t)").bitcast(I32)[:, cols], in_=y_w[:, cols])
 
-        nc.vector.memset(first_s[:].bitcast(I32), 0)
-        nc.vector.memset(second_s[:].bitcast(I32), 0)
-        nc.vector.memset(zero[:], 0.0)
-        nc.vector.memset(third_s[:].bitcast(I32), 0)
+        def pipeline(*stages):
+            for step in range(CHUNKS + len(stages) - 1):
+                for lag, stage in enumerate(stages):
+                    if 0 <= step - lag < CHUNKS:
+                        stage(step - lag)
 
-        load_words(nc.scalar, wa_raw, wa_words)
-        load_words(nc.gpsimd, xt_w, xt_words)
-        load_words(nc.gpsimd, wy_raw, wy_words)
-        load_words(nc.gpsimd, wb_raw, wb_words)
-        nc.scalar.activation(out=th[:, :, PAD - 1:PAD], in_=zero[:, 0:PACK].unsqueeze(2), func=ACT.Tanh)
-        for plane, scales in ((wa_sraw, wa_scales), (xt_s, xt_scales), (wc_sraw, wc_scales)):
-            for q in range(4):
-                load_scales(nc.sync, plane, scales, q)
-        load_words(nc.sync, wc_raw, wc_words)
-        load_words(nc.sync, xq_w, xq_words)
-        for plane, scales in ((xq_s, xq_scales), (wy_sraw, wy_scales)):
-            for q in range(4):
-                load_scales(nc.sync, plane, scales, q)
+        for i in range(4):
+            clear(i)
+        nc.vector.quantize_mx(out=warm_w[:].bitcast(FP8X4), scales=warm_s[:], in_=zeros)
+        for i in range(4, len(widths)):
+            clear(i)
+        for rep in range(WARM_PASSES):
+            nc.tensor.matmul_mx(
+                out=y_ps[LAST][:, 0:CHUNK],
+                lhsT=warm_w[:].bitcast(FP8X4),
+                lhsT_scale=warm_s[:],
+                rhs=warm_w[:].bitcast(U8)[:, 0:2 * CHUNK].bitcast(FP4X4),
+                rhs_scale=warm_s[:],
+                start=True,
+                stop=True,
+            )
+
+        load_fp8_words(nc.scalar, wa_raw, wa_words)
+        load_fp4_words(nc.gpsimd, xt_w, xt_words)
+        load_fp8_words(nc.gpsimd, wy_raw, wy_words)
+        load_fp4_words(nc.gpsimd, wb_raw, wb_words)
+        nc.scalar.activation(out=th[:, :, PAD - 1:PAD], in_=zeros[:, 0:PACK].unsqueeze(2), func=ACT.Tanh)
+        load_scales(wa_sraw, wa_scales)
+        load_scales(xt_s, xt_scales)
+        load_scales(wc_sraw, wc_scales)
+        load_fp8_words(nc.sync, wc_raw, wc_words)
+        load_fp4_words(nc.sync, xq_w, xq_words)
+        load_scales(xq_s, xq_scales)
+        load_scales(wy_sraw, wy_scales)
         nc.sync.dma_start(out=us_sb[:], in_=us.rearrange("(p j) o -> p (j o)", j=PACK))
-        for q in range(4):
-            load_scales(nc.sync, wb_sraw, wb_scales, q)
+        load_scales(wb_sraw, wb_scales)
 
         deal_scales(wa_s, wa_sraw)
-        deal_words(wa_w, wa_raw, 0)
-        deal_words(wa_w, wa_raw, 1)
+        deal_fp8_words(wa_w, wa_raw)
         deal_scales(wc_s, wc_sraw)
-        deal_words(wc_w, wc_raw, 0)
-        deal_words(wy_w, wy_raw, 0)
-        deal_words(wy_w, wy_raw, 1)
+        deal_fp8_words(wc_w, wc_raw)
+        deal_fp8_words(wy_w, wy_raw)
         deal_fp4_words(wb_w, wb_raw)
         deal_scales(wy_s, wy_sraw)
 
-        def tokens_part(c):
-            for z in range(2):
-                fp8_by_fp4(z_ps[c], c, wa_w, wa_s, xt_w, xt_s, z, z == 0, False)
+        for c in range(EARLY):
+            wa_passes(c)
+        for c in range(CHUNKS):
+            if c >= EARLY:
+                wa_passes(c)
+            wc_passes(c)
 
-        def second_input_part(c):
-            fp8_by_fp4(z_ps[c], c, wc_w, wc_s, xq_w, xq_s, 0, False, True)
-            tanh(c)
+        def quantize_hid_for_wb(c):
+            if c == 0:
+                deal_scales(wb_s, wb_sraw)
+            quantize_hid(c)
 
-        def skip(c):
-            for z in range(2):
-                fp8_by_fp4(y_ps[c], c, wy_w, wy_s, xt_w, xt_s, z, z == 0, False)
+        pipeline(tanh, product, round_hid, quantize_hid_for_wb)
 
-        def store_words(c0, c1):
-            cols = slice(c0 * TC, c1 * TC)
-            nc.sync.dma_start(out=out_1.rearrange("z p n t -> p (z n t)").bitcast(I32)[:, cols], in_=y_w[:, cols])
+        for c in range(CHUNKS):
+            wy_passes(c)
+        for c in range(CHUNKS):
+            wb_passes(c)
+        pipeline(drain_y, round_y, quantize_y)
 
-        tokens_part(0)
-        tokens_part(1)
-        second_input_part(0)
-        second_input_part(1)
-        tokens_part(2)
-        second_input_part(2)
-        tokens_part(3)
-        second_input_part(3)
-        product(0)
-        product(1)
-        round_hid(0, True)
-        deal_scales(wb_s, wb_sraw)
-        quantize_hid(0)
-        product(2)
-        round_hid(1)
-        product(3)
-        round_hid(2)
-        quantize_hid(1)
-        round_hid(3, True)
-        skip(0)
-        skip(1)
-        second_layer(0)
-        skip(2)
-        second_layer(1)
-        quantize_hid(2)
-        drain_y(0)
-        quantize_hid(3)
-        drain_y(1)
-        second_layer(2)
-        skip(3)
-        second_layer(3)
-        round_y(0)
-        drain_y(2)
-        round_y(1)
-        quantize_y(0)
-        drain_y(3)
-        round_y(2)
-        quantize_y(1)
-        store_words(0, 2)
-        round_y(3)
-        quantize_y(2)
-        quantize_y(3)
-        store_words(2, 4)
-        for q in range(4):
+        for q in range(QUADRANTS):
             queue = nc.scalar if q % 2 == 0 else nc.sync
             queue.dma_start(
                 out=out_2[0, 4 * q:4 * q + 4, :].bitcast(I32),

from contextlib import ExitStack

import concourse.mybir as mybir

K, L, T, R, N = 1024, 512, 512, 512, 512
FLOPS = 2 * T * (K * R + L * R + R * N + K * N)

F32 = mybir.dt.float32
BF16 = mybir.dt.bfloat16
I32 = mybir.dt.int32
U8 = mybir.dt.uint8
FP8X4 = mybir.dt.float8_e4m3fn_x4
FP4X4 = mybir.dt.float4_e2m1fn_x4
ACT = mybir.ActivationFunctionType
ALU = mybir.AluOpType

P = 128
PACK = 4
QUADRANTS = 4
COLS = 512
CHUNK = 128
CHUNKS = T // CHUNK
LAST = CHUNKS - 1
RUN = 4
PAD = 4
EARLY = 3
WARM_PASSES = 28


def tile_mix_hidden_pairs_multiplied_pl_kernel(
    tc, xt_words, xt_scales, wa_words, wa_scales, xq_words, xq_scales, wc_words, wc_scales, us,
    wb_words, wb_scales, wy_words, wy_scales, out_0, out_1, out_2,
):
    nc = tc.nc
    with ExitStack() as ctx:
        sb = ctx.enter_context(tc.tile_pool(name="sb", bufs=1))
        ps = ctx.enter_context(tc.psum_pool(name="ps", bufs=1))
        ctx.enter_context(tc.manual_schedule())

        def row(name, width, dtype):
            return sb.tile([P, width], dtype, name=name, align_bytes=64)

        xt_w = row("xt_w", 2 * 2 * COLS, U8)
        xq_w = row("xq_w", 2 * COLS, U8)
        wa_raw, wa_w = row("wa_raw", 2 * COLS, I32), row("wa_w", 2 * COLS, I32)
        wc_raw, wc_w = row("wc_raw", COLS, I32), row("wc_w", COLS, I32)
        wy_raw, wy_w = row("wy_raw", 2 * COLS, I32), row("wy_w", 2 * COLS, I32)
        wb_raw, wb_w = row("wb_raw", 2 * COLS, U8), row("wb_w", 2 * COLS, U8)

        widths = [2 * COLS, 2 * COLS, 2 * PACK * CHUNK, 2 * COLS, 2 * COLS, COLS]
        starts = [sum(widths[:i]) for i in range(len(widths) + 1)]
        zeroed = row("zeroed", starts[-1], U8)
        wa_sraw, xt_s, zero_bytes, wc_xq_s, wy_sraw, wb_sraw = [
            zeroed[:, starts[i]:starts[i + 1]] for i in range(len(widths))
        ]
        wc_sraw, xq_s = wc_xq_s[:, 0:COLS], wc_xq_s[:, COLS:2 * COLS]
        zeros = zero_bytes.bitcast(BF16)
        wa_s, wc_s = row("wa_s", 2 * COLS, U8), row("wc_s", COLS, U8)
        wy_s, wb_s = row("wy_s", 2 * COLS, U8), row("wb_s", COLS, U8)
        warm_w, warm_s = row("warm_w", CHUNK, I32), row("warm_s", CHUNK, U8)

        us_sb = row("us_sb", PACK, F32)
        th = sb.tile([P, PACK, PAD + T], F32, name="th", align_bytes=64)
        hid32 = [row("hid32_%d" % c, PACK * CHUNK, F32) for c in range(CHUNKS)]
        hid16 = [row("hid16_%d" % c, PACK * CHUNK, BF16) for c in range(CHUNKS)]
        hid_w = [row("hid_w_%d" % c, CHUNK, I32) for c in range(CHUNKS)]
        hid_s = [row("hid_s_%d" % c, CHUNK, U8) for c in range(CHUNKS)]
        y32 = [row("y32_%d" % c, PACK * CHUNK, F32) for c in range(CHUNKS)]
        y16 = [row("y16_%d" % c, PACK * CHUNK, BF16) for c in range(CHUNKS)]
        y_w, y_s = row("y_w", T, I32), row("y_s", T, U8)
        z_ps = [ps.tile([P, PACK * CHUNK], F32, name="z_ps_%d" % c) for c in range(CHUNKS)]
        y_ps = [ps.tile([P, PACK * CHUNK], F32, name="y_ps_%d" % c) for c in range(CHUNKS)]

        def clear(i):
            first, end = starts[i] // 4 + i % 2, starts[i + 1] // 4 + (i + 1) % 2
            nc.vector.memset(zeroed[:].bitcast(I32)[:, first:end], 0)

        def load_fp8_words(queue, dst, words):
            src = words.rearrange("z p n t -> p z (n t)").bitcast(I32)
            queue.dma_start(out=dst[:].rearrange("p (z n) -> p z n", n=COLS), in_=src)

        def load_fp4_words(queue, dst, words):
            src = words.rearrange("z p b -> p z b").bitcast(I32)
            queue.dma_start(out=dst[:].bitcast(I32).rearrange("p (z n) -> p z n", n=COLS // 2), in_=src)

        def load_scales(plane, scales):
            for q in range(QUADRANTS):
                src = scales[:, 4 * q:4 * q + 4, :].rearrange("z r c -> r z c").bitcast(I32)
                dst = plane.bitcast(I32)[32 * q:32 * q + 4, :].rearrange("r (z c) -> r z c", c=COLS // 4)
                nc.sync.dma_start(out=dst, in_=src)

        def deal_fp8_words(dst, raw):
            for c0 in range(0, raw.shape[1], COLS):
                nc.vector.tensor_copy(
                    out=dst[:, c0:c0 + COLS].rearrange("p (j a b) -> p a j b", j=PACK, b=RUN),
                    in_=raw[:, c0:c0 + COLS].rearrange("p (a b j) -> p a j b", j=PACK, b=RUN),
                )

        def deal_fp4_words(dst, raw):
            nc.vector.tensor_copy(
                out=dst[:].rearrange("p (j m b) -> p j m b", j=PACK, b=2),
                in_=raw[:].rearrange("p (m j b) -> p j m b", j=PACK, b=2),
            )

        def deal_scales(dst, raw):
            nc.vector.tensor_copy(
                out=dst[:].rearrange("p (z j m) -> p z j m", j=PACK, m=P),
                in_=raw.rearrange("p (z m j) -> p z j m", j=PACK, m=P),
            )

        def fp8_weights_by_fp4_tokens(bank, c, w_words, w_scales, x_words, x_scales, opens, closes):
            passes = w_scales.shape[1] // COLS
            for z in range(passes):
                for j in range(PACK):
                    w0, x0 = z * COLS + j * P, z * COLS + c * CHUNK
                    nc.tensor.matmul_mx(
                        out=bank[:, j * CHUNK:(j + 1) * CHUNK],
                        lhsT=w_words[:, w0:w0 + P].bitcast(FP8X4),
                        lhsT_scale=w_scales[:, w0:w0 + P],
                        rhs=x_words[:, 2 * x0:2 * (x0 + CHUNK)].bitcast(FP4X4),
                        rhs_scale=x_scales[:, x0:x0 + CHUNK],
                        start=(opens and z == 0 and j == 0),
                        stop=(closes and z == passes - 1 and j == PACK - 1),
                    )

        def wa_passes(c):
            fp8_weights_by_fp4_tokens(z_ps[c], c, wa_w, wa_s, xt_w, xt_s, True, False)

        def wc_passes(c):
            fp8_weights_by_fp4_tokens(z_ps[c], c, wc_w, wc_s, xq_w, xq_s, False, True)

        def wy_passes(c):
            fp8_weights_by_fp4_tokens(y_ps[c], c, wy_w, wy_s, xt_w, xt_s, True, False)

        def wb_passes(c):
            for j in range(PACK):
                nc.tensor.matmul_mx(
                    out=y_ps[c][:, j * CHUNK:(j + 1) * CHUNK],
                    lhsT=wb_w[:, 2 * j * P:2 * (j + 1) * P].bitcast(FP4X4),
                    lhsT_scale=wb_s[:, j * P:(j + 1) * P],
                    rhs=hid_w[c][:].bitcast(FP8X4),
                    rhs_scale=hid_s[c][:],
                    start=False,
                    stop=(j == PACK - 1),
                )

        def by_row(tile):
            return tile[:].rearrange("p (j t) -> p j t", j=PACK)

        def round_and_interleave(copy, dst16, src32, t0, t1):
            runs = slice(t0 // RUN, t1 // RUN)
            copy(
                out=dst16[:].rearrange("p (a b j) -> p a j b", j=PACK, b=RUN)[:, runs],
                in_=src32[:].rearrange("p (j a b) -> p a j b", j=PACK, b=RUN)[:, runs],
            )

        def tanh(c):
            nc.scalar.activation(out=th[:, :, PAD + c * CHUNK:PAD + (c + 1) * CHUNK], in_=by_row(z_ps[c]), func=ACT.Tanh)

        def product(c):
            for j in range(PACK):
                nc.vector.scalar_tensor_tensor(
                    out=hid32[c][:, j * CHUNK:(j + 1) * CHUNK],
                    in0=z_ps[c][:, j * CHUNK:(j + 1) * CHUNK],
                    scalar=us_sb[:, j:j + 1],
                    in1=th[:, j, PAD - 1 + c * CHUNK:PAD - 1 + (c + 1) * CHUNK],
                    op0=ALU.mult,
                    op1=ALU.mult,
                )

        def round_hid(c):
            copy = nc.vector.tensor_copy if c == LAST else nc.scalar.copy
            round_and_interleave(copy, hid16[c], hid32[c], 0, CHUNK)

        def quantize_hid(c):
            nc.vector.quantize_mx(out=hid_w[c][:].bitcast(FP8X4), scales=hid_s[c][:], in_=hid16[c][:])

        def parts(c):
            return [(0, CHUNK // 2), (CHUNK // 2, CHUNK)] if c == LAST else [(0, CHUNK)]

        def drain_y(c):
            for t0, t1 in parts(c):
                nc.scalar.copy(out=by_row(y32[c])[:, :, t0:t1], in_=by_row(y_ps[c])[:, :, t0:t1])
            rows = out_0.rearrange("(p j) t -> p j t", j=PACK)
            nc.sync.dma_start(out=rows[:, :, c * CHUNK:(c + 1) * CHUNK], in_=by_row(y32[c]))

        def round_y(c):
            for t0, t1 in parts(c):
                round_and_interleave(nc.vector.tensor_copy, y16[c], y32[c], t0, t1)

        def quantize_y(c):
            for t0, t1 in parts(c):
                cols = slice(c * CHUNK + t0, c * CHUNK + t1)
                nc.vector.quantize_mx(
                    out=y_w[:, cols].bitcast(FP8X4), scales=y_s[:, cols], in_=y16[c][:, PACK * t0:PACK * t1]
                )
            if c % 2 == 1:
                cols = slice((c - 1) * CHUNK, (c + 1) * CHUNK)
                nc.sync.dma_start(out=out_1.rearrange("z p n t -> p (z n t)").bitcast(I32)[:, cols], in_=y_w[:, cols])

        def pipeline(*stages):
            for step in range(CHUNKS + len(stages) - 1):
                for lag, stage in enumerate(stages):
                    if 0 <= step - lag < CHUNKS:
                        stage(step - lag)

        for i in range(4):
            clear(i)
        nc.vector.quantize_mx(out=warm_w[:].bitcast(FP8X4), scales=warm_s[:], in_=zeros)
        for i in range(4, len(widths)):
            clear(i)
        for rep in range(WARM_PASSES):
            nc.tensor.matmul_mx(
                out=y_ps[LAST][:, 0:CHUNK],
                lhsT=warm_w[:].bitcast(FP8X4),
                lhsT_scale=warm_s[:],
                rhs=warm_w[:].bitcast(U8)[:, 0:2 * CHUNK].bitcast(FP4X4),
                rhs_scale=warm_s[:],
                start=True,
                stop=True,
            )

        load_fp8_words(nc.scalar, wa_raw, wa_words)
        load_fp4_words(nc.gpsimd, xt_w, xt_words)
        load_fp8_words(nc.gpsimd, wy_raw, wy_words)
        load_fp4_words(nc.gpsimd, wb_raw, wb_words)
        nc.scalar.activation(out=th[:, :, PAD - 1:PAD], in_=zeros[:, 0:PACK].unsqueeze(2), func=ACT.Tanh)
        load_scales(wa_sraw, wa_scales)
        load_scales(xt_s, xt_scales)
        load_scales(wc_sraw, wc_scales)
        load_fp8_words(nc.sync, wc_raw, wc_words)
        load_fp4_words(nc.sync, xq_w, xq_words)
        load_scales(xq_s, xq_scales)
        load_scales(wy_sraw, wy_scales)
        nc.sync.dma_start(out=us_sb[:], in_=us.rearrange("(p j) o -> p (j o)", j=PACK))
        load_scales(wb_sraw, wb_scales)

        deal_scales(wa_s, wa_sraw)
        deal_fp8_words(wa_w, wa_raw)
        deal_scales(wc_s, wc_sraw)
        deal_fp8_words(wc_w, wc_raw)
        deal_fp8_words(wy_w, wy_raw)
        deal_fp4_words(wb_w, wb_raw)
        deal_scales(wy_s, wy_sraw)

        for c in range(EARLY):
            wa_passes(c)
        for c in range(CHUNKS):
            if c >= EARLY:
                wa_passes(c)
            wc_passes(c)

        def quantize_hid_for_wb(c):
            if c == 0:
                deal_scales(wb_s, wb_sraw)
            quantize_hid(c)

        pipeline(tanh, product, round_hid, quantize_hid_for_wb)

        for c in range(CHUNKS):
            wy_passes(c)
        for c in range(CHUNKS):
            wb_passes(c)
        pipeline(drain_y, round_y, quantize_y)

        for q in range(QUADRANTS):
            queue = nc.scalar if q % 2 == 0 else nc.sync
            queue.dma_start(
                out=out_2[0, 4 * q:4 * q + 4, :].bitcast(I32),
                in_=y_s[:].bitcast(I32)[32 * q:32 * q + 4, :],
            )
